import numpy as np
import ml_dtypes


def mxq(x, axis, fmt="e4m3"):
    dtype, down = {"e4m3": (ml_dtypes.float8_e4m3fn, 7), "e5m2": (ml_dtypes.float8_e5m2, 14)}[fmt]
    v = np.moveaxis(np.asarray(x, np.float32).astype(ml_dtypes.bfloat16).astype(np.float64), axis, -1)
    blocks = v.reshape(v.shape[:-1] + (-1, 32))
    amax = np.abs(blocks).max(-1, keepdims=True)
    byte = np.maximum(np.where(amax > 0, np.frexp(amax)[1] - 1 + 127, 0) - down, 1)
    scale = np.exp2(byte - 127.0)
    codes = (blocks / scale).astype(np.float32).astype(dtype).astype(np.float64)
    return np.moveaxis((codes * scale).reshape(v.shape), -1, axis)


WIDE = False


def mx_kscale(k):
    if not WIDE:
        return np.ones(k)
    levels = np.array([10, -10, 5, -5, 0])
    if k % 512:
        return np.exp2(np.random.permutation(np.resize(levels, k // 32))).repeat(32)
    a = np.empty((k // 512, 16))
    for p in range(k // 512):
        a[p, :8] = np.random.permutation(np.resize(levels, 8))
        for g in range(8):
            far = levels[np.abs(levels - a[p, g]) >= 10]
            a[p, g + 8] = far[np.random.randint(len(far))]
    return np.exp2(a.ravel()).repeat(32)


def f64(x):
    return np.asarray(x).astype(np.float64)


def striped(idx):
    return np.tile(idx.reshape(-1, 16).T, (8, 1)).astype(np.uint16)


def unstriped(offs):
    return offs[:16].T.reshape(-1).astype(np.int64)


def pack_weight(w):
    k, n = w.shape
    w = f64(np.asarray(w, np.float32).astype(ml_dtypes.bfloat16)).reshape(k // 32, 32, n)
    amax = np.abs(w).max(1)
    byte = np.clip(np.where(amax > 0, np.frexp(amax)[1] - 1 + 127 - 7, 1), 1, 254)
    scaled = (w * np.exp2(127.0 - byte)[:, None, :]).reshape(k, n).astype(np.float32)
    words = np.ascontiguousarray(scaled.reshape(k // 512, 128, 4, n).transpose(0, 1, 3, 2)).astype(ml_dtypes.float8_e4m3fn).view(np.uint8)
    return words, np.ascontiguousarray(byte.astype(np.uint8).reshape(k // 512, 16, n))


def unpack_weight(words, scales):
    g, p, n, _ = words.shape
    vals = np.ascontiguousarray(words).view(ml_dtypes.float8_e4m3fn).astype(np.float64) * np.repeat(np.exp2(scales.astype(np.float64) - 127.0), 8, axis=1)[..., None]
    return vals.transpose(0, 1, 3, 2).reshape(g * 512, n)


E2M1 = np.array([0.0, 0.5, 1.0, 1.5, 2.0, 3.0, 4.0, 6.0, -0.0, -0.5, -1.0, -1.5, -2.0, -3.0, -4.0, -6.0])


def pack_fp4(w):
    k, n = w.shape
    w = f64(np.asarray(w, np.float32).astype(ml_dtypes.bfloat16)).reshape(k // 32, 32, n)
    amax = np.abs(w).max(1)
    mant, ex = np.frexp(amax / 6.0)
    byte = np.clip(np.where(amax > 0, np.where(mant > 0.5, ex, ex - 1) + 127, 1), 1, 254)
    scaled = (w * np.exp2(127.0 - byte)[:, None, :]).reshape(k, n).astype(np.float32)
    c = np.ascontiguousarray(scaled.reshape(k // 512, 128, 4, n).transpose(0, 1, 3, 2)).astype(ml_dtypes.float4_e2m1fn).view(np.uint8) & 0xF
    words = (c[..., 0::2] | (c[..., 1::2] << 4)).reshape(k // 512, 128, 2 * n)
    return np.ascontiguousarray(words), np.ascontiguousarray(byte.astype(np.uint8).reshape(k // 512, 16, n))


def unpack_fp4(words, scales):
    g, _, n = scales.shape
    words = np.ascontiguousarray(words).reshape(g, 128, n, 2)
    nib = np.empty((g, 128, n, 4), np.uint8)
    nib[..., 0::2] = words & 0xF
    nib[..., 1::2] = words >> 4
    vals = E2M1[nib] * np.repeat(np.exp2(scales.astype(np.float64) - 127.0), 8, axis=1)[..., None]
    return vals.transpose(0, 1, 3, 2).reshape(g * 512, n)


K, T, S, D, N, H, V, U = 512, 2048, 1024, 4, 128, 512, 256, 512


def setup_inputs():
    n = np.random.standard_normal
    s = mx_kscale(K)[:, None]
    u = mx_kscale(H)
    packed_xT = pack_weight(n((K, T)) * s)
    packed_w1 = pack_fp4(n((K, H)) / np.sqrt(K) / s)
    packed_w2 = pack_fp4(n((K, H)) / np.sqrt(K) / s)
    packed_w3 = pack_fp4(n((H, N)) / np.sqrt(H) / u[:, None])
    return {
        "x_words": packed_xT[0],
        "x_scales": packed_xT[1],
        "w1_words": packed_w1[0],
        "w1_scales": packed_w1[1],
        "w2_words": packed_w2[0],
        "w2_scales": packed_w2[1],
        "dtm": (n((H, S))).astype(np.float32),
        "unit": (np.random.uniform(0.6, 1.4, (H, 1)) * u[:, None]).astype(np.float32),
        "w3_words": packed_w3[0],
        "w3_scales": packed_w3[1],
        "offs": striped(np.random.permutation(T)[:S]),
        "ft": striped(np.random.permutation(np.concatenate([np.arange(V), np.random.randint(0, V, U - V)]))),
    }


def reference(x_words, x_scales, w1_words, w1_scales, w2_words, w2_scales, dtm, unit, w3_words, w3_scales, offs, ft):
    xq = unpack_weight(x_words, x_scales)[:, unstriped(offs)]
    gy = unpack_fp4(w2_words, w2_scales).T @ xq
    yy = (gy) ** 2
    syy = yy.reshape(len(yy), -1, D).sum(axis=2) + 0.5
    gx = unpack_fp4(w1_words, w1_scales).T @ xq
    xt = gx * f64(dtm)
    sxt = xt.reshape(len(xt), -1, D).sum(axis=2)
    xy = gx * gy
    sxy = xy.reshape(len(xy), -1, D).sum(axis=2)
    yt = gy * f64(dtm)
    syt = yt.reshape(len(yt), -1, D).sum(axis=2)
    xx = (gx) ** 2
    sxx = xx.reshape(len(xx), -1, D).sum(axis=2) + 0.5
    det = sxx * syy - (0.8 * ((sxy) ** 2)) + 0.3
    u_ = (syy * sxt - (sxy * syt)) / det
    uf = u_[:, unstriped(ft)]
    conf = det / (sxx + syy)
    cf = conf[:, unstriped(ft)]
    hid = f64(unit) * (uf * np.tanh(cf))
    return unpack_fp4(w3_words, w3_scales).T @ mxq(hid, 0, "e4m3")

@@ -1,0 +1,229 @@
+import math
+from contextlib import ExitStack
+
+import concourse.mybir as mybir
+from concourse.masks import make_identity
+
+K, T, S, D, N, H, V, U = 512, 2048, 1024, 4, 128, 512, 256, 512
+FLOPS = 2 * K * H * S * 2 + 2 * H * N * U
+
+F32 = mybir.dt.float32
+BF16 = mybir.dt.bfloat16
+I32 = mybir.dt.int32
+U32 = mybir.dt.uint32
+U16 = mybir.dt.uint16
+U8 = mybir.dt.uint8
+FP8X4 = mybir.dt.float8_e4m3fn_x4
+FP4X4 = mybir.dt.float4_e2m1fn_x4
+ALU = mybir.AluOpType
+ACT = mybir.ActivationFunctionType
+
+P = 128
+PACK = 4
+HALF = 512
+PATCHES = HALF // D
+LINE = 4
+
+
+def load_scale_rows(queue, plane, rows):
+    for q in range(4):
+        queue.dma_start(out=plane[32 * q : 32 * q + 4, :].bitcast(I32), in_=rows[4 * q : 4 * q + 4, :].bitcast(I32))
+
+
+def tile_picked_ylucas_conf_p_kernel(
+    tc, x_words, x_scales, w1_words, w1_scales, w2_words, w2_scales, dtm, unit, w3_words, w3_scales, offs, ft, out
+):
+    nc = tc.nc
+    with ExitStack() as ctx:
+        keep = ctx.enter_context(tc.tile_pool(name="keep", bufs=1))
+        prod = ctx.enter_context(tc.tile_pool(name="prod", bufs=3))
+        small = ctx.enter_context(tc.tile_pool(name="small", bufs=2))
+        psum = ctx.enter_context(tc.psum_pool(name="psum", bufs=1))
+
+        offs_sb = keep.tile([P, S // 16], U16)
+        ft_sb = keep.tile([P, U // 16], U16)
+        xw = keep.tile([P, T], U32, align_bytes=64)
+        xs = keep.tile([P, T], U8, align_bytes=64)
+        w_raw = [keep.tile([P, 2 * H], U8, name="w_raw%d" % i, align_bytes=64) for i in range(2)]
+        ws_raw = [keep.tile([P, H], U8, name="ws_raw%d" % i, align_bytes=64) for i in range(2)]
+        w_dealt = [[keep.tile([P, 2 * P], U8, name="w_dealt%d_%d" % (i, t), align_bytes=64) for t in range(PACK)] for i in range(2)]
+        ws_dealt = [[keep.tile([P, P], U8, name="ws_dealt%d_%d" % (i, t), align_bytes=64) for t in range(PACK)] for i in range(2)]
+        w3w = keep.tile([P, 2 * N], U8, align_bytes=64)
+        w3s = keep.tile([P, N], U8, align_bytes=64)
+        dt_sb = [keep.tile([P, S], F32, name="dt_sb%d" % t) for t in range(PACK)]
+        unit_sb = keep.tile([P, PACK], F32)
+        ident = keep.tile([P, P], F32)
+        one = keep.tile([P, 1], F32)
+        damp = keep.tile([P, 1], F32)
+
+        for plane in (xs, ws_raw[1], ws_raw[0], w3s):
+            nc.vector.memset(plane[:].bitcast(I32), 0)
+        nc.vector.memset(one[:], 1.0)
+        nc.vector.tensor_scalar(damp[:], one[:], -0.3, None, ALU.mult)
+
+        dtm_t = dtm.rearrange("(p t) j -> t p j", t=PACK)
+        nc.sync.dma_start(out=xw[:].bitcast(I32), in_=x_words[0].rearrange("p c r -> p (c r)").bitcast(I32))
+        nc.sync.dma_start(offs_sb[:], offs)
+        nc.scalar.dma_start(out=w_raw[1][:].bitcast(I32), in_=w2_words[0].bitcast(I32))
+        nc.scalar.dma_start(out=w_raw[0][:].bitcast(I32), in_=w1_words[0].bitcast(I32))
+        load_scale_rows(nc.sync, xs, x_scales[0])
+        load_scale_rows(nc.scalar, ws_raw[1], w2_scales[0])
+        load_scale_rows(nc.gpsimd, ws_raw[0], w1_scales[0])
+        make_identity(nc, ident[:])
+        for t in range(PACK):
+            nc.sync.dma_start(out=dt_sb[t][:], in_=dtm_t[t])
+        nc.sync.dma_start(out=unit_sb[:], in_=unit.rearrange("(p t) o -> p (t o)", t=PACK))
+        nc.sync.dma_start(ft_sb[:], ft)
+        nc.sync.dma_start(out=w3w[:].bitcast(I32), in_=w3_words[0].bitcast(I32))
+        load_scale_rows(nc.sync, w3s, w3_scales[0])
+
+        def deal(engine, t):
+            for i in (1, 0):
+                engine.tensor_copy(
+                    out=w_dealt[i][t][:].rearrange("p (m b) -> p m b", b=2),
+                    in_=w_raw[i][:].rearrange("p (m t b) -> p t m b", t=PACK, b=2)[:, t],
+                )
+                engine.tensor_copy(out=ws_dealt[i][t][:], in_=ws_raw[i][:].rearrange("p (m t) -> p t m", t=PACK)[:, t])
+
+        xg = [keep.tile([P, HALF], U32, name="xg%d" % h, align_bytes=64) for h in range(2)]
+        sg = [keep.tile([P, HALF], U8, name="sg%d" % h, align_bytes=64) for h in range(2)]
+        deal(nc.vector, 0)
+        for h in range(2):
+            piece = offs_sb[:, h * (HALF // 16) : (h + 1) * (HALF // 16)]
+            nc.vector.tensor_copy(xg[h][:], xw[:].indirect(piece))
+            nc.vector.tensor_copy(sg[h][:], xs[:].indirect(piece))
+        for t in range(1, PACK):
+            deal(nc.gpsimd, t)
+
+        def gradient(i, t, h, bank):
+            nc.tensor.matmul_mx(
+                out=bank[:],
+                lhsT=w_dealt[i][t][:].bitcast(FP4X4),
+                lhsT_scale=ws_dealt[i][t][:],
+                rhs=xg[h][:].bitcast(FP8X4),
+                rhs_scale=sg[h][:],
+                start=True,
+                stop=True,
+            )
+
+        def turn_and_add(dst, terms):
+            for n, term in enumerate(terms):
+                nc.tensor.matmul(dst, term, ident[:], start=(n == 0), stop=(n == len(terms) - 1), is_transpose=True)
+
+        def by_member(ap):
+            return ap.rearrange("p (v d) -> p d v", d=D)
+
+        def by_line_natural(ap):
+            return ap.rearrange("p (c i d) -> p c d i", i=LINE, d=D)
+
+        def by_line_split(ap):
+            return ap.rearrange("p d (c i) -> p c d i", i=LINE)
+
+        neg_conf = keep.tile([P, PACK, V], F32)
+        table = [keep.tile([P, 4 * V], F32, name="table%d" % t) for t in range(PACK)]
+
+        def gradients(step):
+            t, h = divmod(step, 2)
+            gy = psum.tile([P, HALF], F32, tag="gy")
+            gx = psum.tile([P, HALF], F32, tag="gx", bufs=2)
+            gradient(1, t, h, gy)
+            gradient(0, t, h, gx)
+            return gx, gy
+
+        gx, gy = gradients(0)
+        for t in range(PACK):
+            sums_x = psum.tile([P, 2, V], F32, tag="sums_x")
+            sums_sq = psum.tile([P, 2, V], F32, tag="sums_sq")
+            sums_yt = psum.tile([P, V], F32, tag="sums_yt")
+            for h in range(2):
+                dt_half = dt_sb[t][:, h * HALF : (h + 1) * HALF]
+                y_sb = prod.tile([P, D, PATCHES], F32)
+                xt = prod.tile([P, D, PATCHES], F32)
+                yy = prod.tile([P, D, PATCHES], F32)
+                xy = prod.tile([P, D, PATCHES], F32)
+                xx = prod.tile([P, D, PATCHES], F32)
+                yt = prod.tile([P, D, PATCHES], F32)
+                nc.scalar.copy(y_sb[:], by_member(gy[:]))
+                nc.vector.tensor_tensor(by_line_split(xt[:]), by_line_natural(gx[:]), by_line_natural(dt_half), ALU.mult)
+                nc.scalar.activation(yy[:], by_member(gy[:]), ACT.Square)
+                nc.vector.tensor_tensor(xy[:], by_member(gx[:]), y_sb[:], ALU.mult)
+                nc.scalar.activation(xx[:], by_member(gx[:]), ACT.Square)
+                nc.vector.tensor_tensor(by_line_split(yt[:]), by_line_split(y_sb[:]), by_line_natural(dt_half), ALU.mult)
+                if 2 * t + h + 1 < 2 * PACK:
+                    gx, gy = gradients(2 * t + h + 1)
+                cols = slice(h * P, (h + 1) * P)
+                for dst, src in (
+                    (sums_x[:, 0, cols], xt),
+                    (sums_sq[:, 0, cols], yy),
+                    (sums_x[:, 1, cols], xy),
+                    (sums_sq[:, 1, cols], xx),
+                    (sums_yt[:, cols], yt),
+                ):
+                    turn_and_add(dst, [src[:, d, :] for d in range(D)])
+
+            sxy = small.tile([P, V], F32)
+            damped = small.tile([P, V], F32)
+            neg_syy = small.tile([P, V], F32)
+            neg_n1 = small.tile([P, V], F32)
+            neg_ab = small.tile([P, V], F32)
+            trace = small.tile([P, V], F32)
+            n2 = small.tile([P, V], F32)
+            nc.scalar.copy(sxy[:], sums_x[:, 1, :])
+            nc.scalar.activation(damped[:], sums_x[:, 1, :], ACT.Square, scale=math.sqrt(0.8))
+            nc.scalar.activation(neg_syy[:], sums_sq[:, 0, :], ACT.Copy, bias=-0.5, scale=-1.0)
+            nc.vector.tensor_tensor(neg_n1[:], sums_x[:, 0, :], neg_syy[:], ALU.mult)
+            nc.vector.scalar_tensor_tensor(neg_ab[:], sums_sq[:, 1, :], 0.5, neg_syy[:], ALU.add, ALU.mult)
+            nc.vector.scalar_tensor_tensor(trace[:], sums_sq[:, 1, :], 0.8, neg_syy[:], ALU.add, ALU.subtract)
+            nc.vector.tensor_tensor(n2[:], sums_yt[:], sxy[:], ALU.mult)
+
+            det_tr = psum.tile([P, 2, V], F32, tag="det_tr")
+            neg_num = psum.tile([P, V], F32, tag="neg_num")
+            for h in range(2):
+                cols = slice(h * P, (h + 1) * P)
+                turn_and_add(det_tr[:, 0, cols], [neg_ab[:, cols], damped[:, cols]])
+                turn_and_add(det_tr[:, 1, cols], [trace[:, cols]])
+            for h in range(2):
+                cols = slice(h * P, (h + 1) * P)
+                turn_and_add(neg_num[:, cols], [neg_n1[:, cols], n2[:, cols]])
+
+            root = small.tile([P, 2 * V], F32, tag="root", bufs=1)
+            neg_u = table[t][:, V : 2 * V]
+            inv = table[t][:, 2 * V : 4 * V]
+            nc.scalar.activation(root[:], det_tr[:].rearrange("p a v -> p (a v)"), ACT.Abs_reciprocal_sqrt, bias=damp[:])
+            nc.scalar.activation(inv, root[:], ACT.Square)
+            nc.vector.scalar_tensor_tensor(neg_conf[:, t, :], det_tr[:, 0, :], -0.3, inv[:, V : 2 * V], ALU.add, ALU.mult)
+            nc.vector.scalar_tensor_tensor(neg_u, neg_num[:], unit_sb[:, t : t + 1], inv[:, 0:V], ALU.mult, ALU.mult)
+
+        neg_tanh = small.tile([P, PACK, V], F32, tag="root", bufs=1)
+        for t in range(PACK):
+            nc.scalar.activation(neg_tanh[:, t, :], neg_conf[:, t, :], ACT.Tanh)
+            nc.vector.tensor_tensor(table[t][:, 0:V], table[t][:, V : 2 * V], neg_tanh[:, t, :], ALU.mult)
+
+        width = U // 2
+        for r in range(2):
+            piece = ft_sb[:, r * (width // 16) : (r + 1) * (width // 16)]
+            planes = small.tile([P, PACK, width], BF16)
+            for t in range(PACK - 1):
+                nc.scalar.activation(planes[:, t, :], table[t][:].indirect(piece), ACT.Copy)
+            nc.vector.tensor_copy(planes[:, PACK - 1, :], table[PACK - 1][:].indirect(piece))
+            woven = small.tile([P, width, PACK], BF16, align_bytes=64)
+            nc.vector.tensor_copy(
+                out=woven[:].rearrange("p (c i) t -> p c t i", i=4),
+                in_=planes[:].rearrange("p t (c i) -> p c t i", i=4),
+            )
+            codes = small.tile([P, width], U32, align_bytes=64)
+            scales = small.tile([P, width], U8, align_bytes=64)
+            nc.vector.quantize_mx(out=codes[:].bitcast(FP8X4), scales=scales[:], in_=woven[:].rearrange("p c t -> p (c t)"))
+            motion = psum.tile([P, HALF], F32, tag="gx", bufs=2)
+            nc.tensor.matmul_mx(
+                out=motion[:, 0:width],
+                lhsT=w3w[:].bitcast(FP4X4),
+                lhsT_scale=w3s[:],
+                rhs=codes[:].bitcast(FP8X4),
+                rhs_scale=scales[:],
+                start=True,
+                stop=True,
+            )
+            result = small.tile([P, width], F32)
+            nc.scalar.copy(result[:], motion[:, 0:width])
+            nc.sync.dma_start(out=out[:, r * width : (r + 1) * width], in_=result[:])

@@ -25,8 +25,8 @@ PATCHES = HALF // D
 LINE = 4
 
 
-def load_scale_rows(queue, plane, rows):
-    for q in range(4):
+def load_scale_rows(queues, plane, rows):
+    for q, queue in enumerate(queues):
         queue.dma_start(out=plane[32 * q : 32 * q + 4, :].bitcast(I32), in_=rows[4 * q : 4 * q + 4, :].bitcast(I32))
 
 
@@ -36,70 +36,69 @@ def tile_picked_ylucas_conf_p_kernel(
     nc = tc.nc
     with ExitStack() as ctx:
         keep = ctx.enter_context(tc.tile_pool(name="keep", bufs=1))
+        stream = ctx.enter_context(tc.tile_pool(name="stream", bufs=3))
         prod = ctx.enter_context(tc.tile_pool(name="prod", bufs=3))
-        small = ctx.enter_context(tc.tile_pool(name="small", bufs=2))
+        small = ctx.enter_context(tc.tile_pool(name="small", bufs=3))
         psum = ctx.enter_context(tc.psum_pool(name="psum", bufs=1))
 
         offs_sb = keep.tile([P, S // 16], U16)
         ft_sb = keep.tile([P, U // 16], U16)
         xw = keep.tile([P, T], U32, align_bytes=64)
         xs = keep.tile([P, T], U8, align_bytes=64)
-        w_raw = [keep.tile([P, 2 * H], U8, name="w_raw%d" % i, align_bytes=64) for i in range(2)]
-        ws_raw = [keep.tile([P, H], U8, name="ws_raw%d" % i, align_bytes=64) for i in range(2)]
-        w_dealt = [[keep.tile([P, 2 * P], U8, name="w_dealt%d_%d" % (i, t), align_bytes=64) for t in range(PACK)] for i in range(2)]
-        ws_dealt = [[keep.tile([P, P], U8, name="ws_dealt%d_%d" % (i, t), align_bytes=64) for t in range(PACK)] for i in range(2)]
-        w3w = keep.tile([P, 2 * N], U8, align_bytes=64)
-        w3s = keep.tile([P, N], U8, align_bytes=64)
-        dt_sb = [keep.tile([P, S], F32, name="dt_sb%d" % t) for t in range(PACK)]
+        w2_raw = stream.tile([P, 2 * H], U8, tag="stream", align_bytes=64)
+        w1_raw = stream.tile([P, 2 * H], U8, tag="stream", align_bytes=64)
+        s1_raw = stream.tile([P, H], U8, tag="stream", align_bytes=64)
+        s2_raw = keep.tile([P, H], U8, align_bytes=64)
+        w_raw = [w1_raw, w2_raw]
+        ws_raw = [s1_raw, s2_raw]
+        w_dealt = [keep.tile([P, 2 * H], U8, name="w_dealt%d" % i, align_bytes=64) for i in range(2)]
+        ws_dealt = [keep.tile([P, H], U8, name="ws_dealt%d" % i, align_bytes=64) for i in range(2)]
         unit_sb = keep.tile([P, PACK], F32)
         ident = keep.tile([P, P], F32)
         one = keep.tile([P, 1], F32)
         damp = keep.tile([P, 1], F32)
 
-        for plane in (xs, ws_raw[1], ws_raw[0], w3s):
+        nc.gpsimd.memset(xs[:].bitcast(I32), 0)
+        for plane in (s2_raw, s1_raw):
             nc.vector.memset(plane[:].bitcast(I32), 0)
         nc.vector.memset(one[:], 1.0)
         nc.vector.tensor_scalar(damp[:], one[:], -0.3, None, ALU.mult)
 
         dtm_t = dtm.rearrange("(p t) j -> t p j", t=PACK)
-        nc.sync.dma_start(out=xw[:].bitcast(I32), in_=x_words[0].rearrange("p c r -> p (c r)").bitcast(I32))
         nc.sync.dma_start(offs_sb[:], offs)
-        nc.scalar.dma_start(out=w_raw[1][:].bitcast(I32), in_=w2_words[0].bitcast(I32))
-        nc.scalar.dma_start(out=w_raw[0][:].bitcast(I32), in_=w1_words[0].bitcast(I32))
-        load_scale_rows(nc.sync, xs, x_scales[0])
-        load_scale_rows(nc.scalar, ws_raw[1], w2_scales[0])
-        load_scale_rows(nc.gpsimd, ws_raw[0], w1_scales[0])
+        nc.scalar.dma_start(out=w2_raw[:].bitcast(I32), in_=w2_words[0].bitcast(I32))
+        nc.sync.dma_start(out=xw[:].bitcast(I32), in_=x_words[0].rearrange("p c r -> p (c r)").bitcast(I32))
+        nc.scalar.dma_start(out=w1_raw[:].bitcast(I32), in_=w1_words[0].bitcast(I32))
+        load_scale_rows((nc.sync,) * 4, xs[:], x_scales[0])
+        load_scale_rows((nc.scalar,) * 4, s2_raw[:], w2_scales[0])
+        load_scale_rows((nc.sync, nc.scalar, nc.sync, nc.scalar), s1_raw[:], w1_scales[0])
         make_identity(nc, ident[:])
-        for t in range(PACK):
-            nc.sync.dma_start(out=dt_sb[t][:], in_=dtm_t[t])
-        nc.sync.dma_start(out=unit_sb[:], in_=unit.rearrange("(p t) o -> p (t o)", t=PACK))
-        nc.sync.dma_start(ft_sb[:], ft)
-        nc.sync.dma_start(out=w3w[:].bitcast(I32), in_=w3_words[0].bitcast(I32))
-        load_scale_rows(nc.sync, w3s, w3_scales[0])
+        nc.gpsimd.dma_start(out=unit_sb[:], in_=unit.rearrange("(p t) o -> p (t o)", t=PACK))
 
-        def deal(engine, t):
-            for i in (1, 0):
-                engine.tensor_copy(
-                    out=w_dealt[i][t][:].rearrange("p (m b) -> p m b", b=2),
-                    in_=w_raw[i][:].rearrange("p (m t b) -> p t m b", t=PACK, b=2)[:, t],
-                )
-                engine.tensor_copy(out=ws_dealt[i][t][:], in_=ws_raw[i][:].rearrange("p (m t) -> p t m", t=PACK)[:, t])
+        for i in (1, 0):
+            nc.vector.tensor_copy(
+                out=w_dealt[i][:].rearrange("p (t m b) -> p t m b", t=PACK, b=2),
+                in_=w_raw[i][:].rearrange("p (m t b) -> p t m b", t=PACK, b=2),
+            )
+        for i in (1, 0):
+            nc.vector.tensor_copy(
+                out=ws_dealt[i][:].rearrange("p (t m) -> p t m", t=PACK),
+                in_=ws_raw[i][:].rearrange("p (m t) -> p t m", t=PACK),
+            )
 
         xg = [keep.tile([P, HALF], U32, name="xg%d" % h, align_bytes=64) for h in range(2)]
         sg = [keep.tile([P, HALF], U8, name="sg%d" % h, align_bytes=64) for h in range(2)]
-        deal(nc.vector, 0)
         for h in range(2):
             piece = offs_sb[:, h * (HALF // 16) : (h + 1) * (HALF // 16)]
-            nc.vector.tensor_copy(xg[h][:], xw[:].indirect(piece))
             nc.vector.tensor_copy(sg[h][:], xs[:].indirect(piece))
-        for t in range(1, PACK):
-            deal(nc.gpsimd, t)
+            nc.vector.tensor_copy(xg[h][:], xw[:].indirect(piece))
+
 
         def gradient(i, t, h, bank):
             nc.tensor.matmul_mx(
                 out=bank[:],
-                lhsT=w_dealt[i][t][:].bitcast(FP4X4),
-                lhsT_scale=ws_dealt[i][t][:],
+                lhsT=w_dealt[i][:, 2 * P * t : 2 * P * (t + 1)].bitcast(FP4X4),
+                lhsT_scale=ws_dealt[i][:, P * t : P * (t + 1)],
                 rhs=xg[h][:].bitcast(FP8X4),
                 rhs_scale=sg[h][:],
                 start=True,
@@ -122,77 +121,112 @@ def tile_picked_ylucas_conf_p_kernel(
         neg_conf = keep.tile([P, PACK, V], F32)
         table = [keep.tile([P, 4 * V], F32, name="table%d" % t) for t in range(PACK)]
 
+        steps = 2 * PACK
+        st = [dict() for step in range(steps)]
+
+        def load_dt(step):
+            t, h = divmod(step, 2)
+            dt_half = stream.tile([P, HALF], F32, tag="stream", align_bytes=64)
+            nc.sync.dma_start(out=dt_half[:], in_=dtm_t[t, :, h * HALF : (h + 1) * HALF])
+            st[step].update(dt=dt_half[:])
+
         def gradients(step):
             t, h = divmod(step, 2)
             gy = psum.tile([P, HALF], F32, tag="gy")
             gx = psum.tile([P, HALF], F32, tag="gx", bufs=2)
             gradient(1, t, h, gy)
             gradient(0, t, h, gx)
-            return gx, gy
+            st[step].update(gx=gx, gy=gy)
 
-        gx, gy = gradients(0)
-        for t in range(PACK):
-            sums_x = psum.tile([P, 2, V], F32, tag="sums_x")
-            sums_sq = psum.tile([P, 2, V], F32, tag="sums_sq")
-            sums_yt = psum.tile([P, V], F32, tag="sums_yt")
-            for h in range(2):
-                dt_half = dt_sb[t][:, h * HALF : (h + 1) * HALF]
-                y_sb = prod.tile([P, D, PATCHES], F32)
-                xt = prod.tile([P, D, PATCHES], F32)
-                yy = prod.tile([P, D, PATCHES], F32)
-                xy = prod.tile([P, D, PATCHES], F32)
-                xx = prod.tile([P, D, PATCHES], F32)
-                yt = prod.tile([P, D, PATCHES], F32)
-                nc.scalar.copy(y_sb[:], by_member(gy[:]))
-                nc.vector.tensor_tensor(by_line_split(xt[:]), by_line_natural(gx[:]), by_line_natural(dt_half), ALU.mult)
-                nc.scalar.activation(yy[:], by_member(gy[:]), ACT.Square)
-                nc.vector.tensor_tensor(xy[:], by_member(gx[:]), y_sb[:], ALU.mult)
-                nc.scalar.activation(xx[:], by_member(gx[:]), ACT.Square)
-                nc.vector.tensor_tensor(by_line_split(yt[:]), by_line_split(y_sb[:]), by_line_natural(dt_half), ALU.mult)
-                if 2 * t + h + 1 < 2 * PACK:
-                    gx, gy = gradients(2 * t + h + 1)
-                cols = slice(h * P, (h + 1) * P)
-                for dst, src in (
-                    (sums_x[:, 0, cols], xt),
-                    (sums_sq[:, 0, cols], yy),
-                    (sums_x[:, 1, cols], xy),
-                    (sums_sq[:, 1, cols], xx),
-                    (sums_yt[:, cols], yt),
-                ):
-                    turn_and_add(dst, [src[:, d, :] for d in range(D)])
+        def products(step):
+            gx, gy, dt_half = st[step]["gx"], st[step]["gy"], st[step]["dt"]
+            y_sb = prod.tile([P, D, PATCHES], F32)
+            xt = prod.tile([P, D, PATCHES], F32)
+            yy = prod.tile([P, D, PATCHES], F32)
+            xy = prod.tile([P, D, PATCHES], F32)
+            xx = prod.tile([P, D, PATCHES], F32)
+            yt = prod.tile([P, D, PATCHES], F32)
+            nc.scalar.copy(y_sb[:], by_member(gy[:]))
+            nc.vector.tensor_tensor(by_line_split(xt[:]), by_line_natural(gx[:]), by_line_natural(dt_half), ALU.mult)
+            nc.gpsimd.tensor_tensor(yy[:], y_sb[:], y_sb[:], ALU.mult)
+            nc.scalar.activation(xx[:], by_member(gx[:]), ACT.Square)
+            nc.vector.tensor_tensor(xy[:], by_member(gx[:]), y_sb[:], ALU.mult)
+            nc.gpsimd.tensor_tensor(by_line_split(yt[:]), by_line_split(y_sb[:]), by_line_natural(dt_half), ALU.mult)
+            st[step].update(xt=xt, yy=yy, xy=xy, xx=xx, yt=yt)
 
-            sxy = small.tile([P, V], F32)
-            damped = small.tile([P, V], F32)
-            neg_syy = small.tile([P, V], F32)
-            neg_n1 = small.tile([P, V], F32)
-            neg_ab = small.tile([P, V], F32)
-            trace = small.tile([P, V], F32)
-            n2 = small.tile([P, V], F32)
-            nc.scalar.copy(sxy[:], sums_x[:, 1, :])
-            nc.scalar.activation(damped[:], sums_x[:, 1, :], ACT.Square, scale=math.sqrt(0.8))
-            nc.scalar.activation(neg_syy[:], sums_sq[:, 0, :], ACT.Copy, bias=-0.5, scale=-1.0)
-            nc.vector.tensor_tensor(neg_n1[:], sums_x[:, 0, :], neg_syy[:], ALU.mult)
-            nc.vector.scalar_tensor_tensor(neg_ab[:], sums_sq[:, 1, :], 0.5, neg_syy[:], ALU.add, ALU.mult)
-            nc.vector.scalar_tensor_tensor(trace[:], sums_sq[:, 1, :], 0.8, neg_syy[:], ALU.add, ALU.subtract)
-            nc.vector.tensor_tensor(n2[:], sums_yt[:], sxy[:], ALU.mult)
+        def patch_sums(step):
+            sums = psum.tile([P, 4, P], F32, tag="sums", bufs=2)
+            s_yt = psum.tile([P, P], F32, tag="s_yt")
+            for n, name in enumerate(("xt", "xx", "yy", "xy")):
+                turn_and_add(sums[:, n, :], [st[step][name][:, d, :] for d in range(D)])
+            turn_and_add(s_yt[:], [st[step]["yt"][:, d, :] for d in range(D)])
+            st[step].update(s_xt=sums[:, 0, :], s_xx=sums[:, 1, :], s_yy=sums[:, 2, :], s_xy=sums[:, 3, :], s_yt=s_yt[:])
 
-            det_tr = psum.tile([P, 2, V], F32, tag="det_tr")
-            neg_num = psum.tile([P, V], F32, tag="neg_num")
-            for h in range(2):
-                cols = slice(h * P, (h + 1) * P)
-                turn_and_add(det_tr[:, 0, cols], [neg_ab[:, cols], damped[:, cols]])
-                turn_and_add(det_tr[:, 1, cols], [trace[:, cols]])
-            for h in range(2):
-                cols = slice(h * P, (h + 1) * P)
-                turn_and_add(neg_num[:, cols], [neg_n1[:, cols], n2[:, cols]])
+        def factors(step):
+            sxy = small.tile([P, P], F32)
+            damped = small.tile([P, P], F32)
+            neg_syy = small.tile([P, P], F32)
+            nc.scalar.activation(neg_syy[:], st[step]["s_yy"], ACT.Copy, bias=-0.5, scale=-1.0)
+            nc.scalar.activation(damped[:], st[step]["s_xy"], ACT.Square, scale=math.sqrt(0.8))
+            nc.scalar.copy(sxy[:], st[step]["s_xy"])
+            st[step].update(sxy=sxy, damped=damped, neg_syy=neg_syy)
 
-            root = small.tile([P, 2 * V], F32, tag="root", bufs=1)
-            neg_u = table[t][:, V : 2 * V]
-            inv = table[t][:, 2 * V : 4 * V]
-            nc.scalar.activation(root[:], det_tr[:].rearrange("p a v -> p (a v)"), ACT.Abs_reciprocal_sqrt, bias=damp[:])
-            nc.scalar.activation(inv, root[:], ACT.Square)
-            nc.vector.scalar_tensor_tensor(neg_conf[:, t, :], det_tr[:, 0, :], -0.3, inv[:, V : 2 * V], ALU.add, ALU.mult)
-            nc.vector.scalar_tensor_tensor(neg_u, neg_num[:], unit_sb[:, t : t + 1], inv[:, 0:V], ALU.mult, ALU.mult)
+        def terms(step):
+            neg_n1 = small.tile([P, P], F32)
+            neg_ab = small.tile([P, P], F32)
+            trace = small.tile([P, P], F32)
+            n2 = small.tile([P, P], F32)
+            neg_syy = st[step]["neg_syy"]
+            nc.vector.scalar_tensor_tensor(neg_ab[:], st[step]["s_xx"], 0.5, neg_syy[:], ALU.add, ALU.mult)
+            nc.vector.scalar_tensor_tensor(trace[:], st[step]["s_xx"], 0.8, neg_syy[:], ALU.add, ALU.subtract)
+            nc.vector.tensor_tensor(neg_n1[:], st[step]["s_xt"], neg_syy[:], ALU.mult)
+            nc.vector.tensor_tensor(n2[:], st[step]["s_yt"], st[step]["sxy"][:], ALU.mult)
+            st[step].update(neg_n1=neg_n1, neg_ab=neg_ab, trace=trace, n2=n2)
+
+        def turn_back(step):
+            back = psum.tile([P, 3, P], F32, tag="back", bufs=2)
+            turn_and_add(back[:, 0, :], [st[step]["neg_ab"][:], st[step]["damped"][:]])
+            turn_and_add(back[:, 1, :], [st[step]["trace"][:]])
+            turn_and_add(back[:, 2, :], [st[step]["neg_n1"][:], st[step]["n2"][:]])
+            st[step].update(back=back)
+
+        def inverses(step):
+            t, h = divmod(step, 2)
+            root = small.tile([P, 2, P], F32, tag="root", bufs=1)
+            nc.scalar.activation(root[:], st[step]["back"][:, 0:2, :], ACT.Abs_reciprocal_sqrt, bias=damp[:])
+            nc.scalar.activation(table[t][:, (2 + h) * V : (3 + h) * V], root[:].rearrange("p a v -> p (a v)"), ACT.Square)
+
+        def quotients(step):
+            t, h = divmod(step, 2)
+            back = st[step]["back"]
+            inv = table[t][:, (2 + h) * V : (3 + h) * V]
+            neg_u = table[t][:, V + h * P : V + (h + 1) * P]
+            nc.vector.scalar_tensor_tensor(neg_conf[:, t, h * P : (h + 1) * P], back[:, 0, :], -0.3, inv[:, P : 2 * P], ALU.add, ALU.mult)
+            nc.vector.scalar_tensor_tensor(neg_u, back[:, 2, :], unit_sb[:, t : t + 1], inv[:, 0:P], ALU.mult, ALU.mult)
+
+        load_dt(0)
+        load_dt(1)
+        stages = (
+            (load_dt, -2),
+            (gradients, 0),
+            (inverses, 3),
+            (terms, 2),
+            (products, 0),
+            (quotients, 3),
+            (patch_sums, 1),
+            (turn_back, 2),
+            (factors, 1),
+        )
+        for turn in range(steps + 3):
+            for stage, lag in stages:
+                if 0 <= turn - lag < steps:
+                    stage(turn - lag)
+
+        nc.sync.dma_start(ft_sb[:], ft)
+        w3s = s2_raw[:, 0:N]
+        load_scale_rows((nc.sync,) * 4, w3s, w3_scales[0])
+        w3w = stream.tile([P, 2 * N], U8, tag="stream", align_bytes=64)
+        nc.sync.dma_start(out=w3w[:].bitcast(I32), in_=w3_words[0].bitcast(I32))
 
         neg_tanh = small.tile([P, PACK, V], F32, tag="root", bufs=1)
         for t in range(PACK):
@@ -218,7 +252,7 @@ def tile_picked_ylucas_conf_p_kernel(
             nc.tensor.matmul_mx(
                 out=motion[:, 0:width],
                 lhsT=w3w[:].bitcast(FP4X4),
-                lhsT_scale=w3s[:],
+                lhsT_scale=w3s,
                 rhs=codes[:].bitcast(FP8X4),
                 rhs_scale=scales[:],
                 start=True,

@@ -23,6 +23,7 @@ PACK = 4
 HALF = 512
 PATCHES = HALF // D
 LINE = 4
+YT_ON_VECTOR = 32
 
 
 def load_scale_rows(queues, plane, rows):
@@ -47,15 +48,15 @@ def tile_picked_ylucas_conf_p_kernel(
         xs = keep.tile([P, T], U8, align_bytes=64)
         w2_raw = stream.tile([P, 2 * H], U8, tag="stream", align_bytes=64)
         w1_raw = stream.tile([P, 2 * H], U8, tag="stream", align_bytes=64)
-        s1_raw = stream.tile([P, H], U8, tag="stream", align_bytes=64)
-        s2_raw = keep.tile([P, H], U8, align_bytes=64)
+        one = stream.tile([P, 1], F32, tag="stream", align_bytes=64)
+        s1_raw = keep.tile([P, H], U8, tag="late_words", align_bytes=64)
+        s2_raw = keep.tile([P, H], U8, tag="late_bytes", align_bytes=64)
         w_raw = [w1_raw, w2_raw]
         ws_raw = [s1_raw, s2_raw]
         w_dealt = [keep.tile([P, 2 * H], U8, name="w_dealt%d" % i, align_bytes=64) for i in range(2)]
         ws_dealt = [keep.tile([P, H], U8, name="ws_dealt%d" % i, align_bytes=64) for i in range(2)]
         unit_sb = keep.tile([P, PACK], F32)
         ident = keep.tile([P, P], F32)
-        one = keep.tile([P, 1], F32)
         damp = keep.tile([P, 1], F32)
 
         nc.gpsimd.memset(xs[:].bitcast(I32), 0)
@@ -86,8 +87,8 @@ def tile_picked_ylucas_conf_p_kernel(
                 in_=ws_raw[i][:].rearrange("p (m t) -> p t m", t=PACK),
             )
 
-        xg = [keep.tile([P, HALF], U32, name="xg%d" % h, align_bytes=64) for h in range(2)]
-        sg = [keep.tile([P, HALF], U8, name="sg%d" % h, align_bytes=64) for h in range(2)]
+        xg = [keep.tile([P, HALF], U32, name="xg", tag=tag, align_bytes=64) for tag in ("first_words", "late_words")]
+        sg = [keep.tile([P, HALF], U8, name="sg", tag=tag, align_bytes=64) for tag in ("first_bytes", "late_bytes")]
         for h in range(2):
             piece = offs_sb[:, h * (HALF // 16) : (h + 1) * (HALF // 16)]
             nc.vector.tensor_copy(sg[h][:], xs[:].indirect(piece))
@@ -138,29 +139,46 @@ def tile_picked_ylucas_conf_p_kernel(
             gradient(0, t, h, gx)
             st[step].update(gx=gx, gy=gy)
 
-        def products(step):
+        def first_products(step):
             gx, gy, dt_half = st[step]["gx"], st[step]["gy"], st[step]["dt"]
             y_sb = prod.tile([P, D, PATCHES], F32)
             xt = prod.tile([P, D, PATCHES], F32)
             yy = prod.tile([P, D, PATCHES], F32)
-            xy = prod.tile([P, D, PATCHES], F32)
-            xx = prod.tile([P, D, PATCHES], F32)
             yt = prod.tile([P, D, PATCHES], F32)
             nc.scalar.copy(y_sb[:], by_member(gy[:]))
             nc.vector.tensor_tensor(by_line_split(xt[:]), by_line_natural(gx[:]), by_line_natural(dt_half), ALU.mult)
-            nc.gpsimd.tensor_tensor(yy[:], y_sb[:], y_sb[:], ALU.mult)
+            nc.scalar.activation(yy[:, 0:1, :], by_member(gy[:])[:, 0:1, :], ACT.Square)
+            nc.gpsimd.tensor_tensor(yy[:, 1:D, :], y_sb[:, 1:D, :], y_sb[:, 1:D, :], ALU.mult)
+            cut = D * YT_ON_VECTOR
+            nc.vector.tensor_tensor(
+                by_line_split(yt[:, :, 0:YT_ON_VECTOR]), by_line_natural(gy[:, 0:cut]), by_line_natural(dt_half[:, 0:cut]), ALU.mult
+            )
+            nc.gpsimd.tensor_tensor(
+                by_line_split(yt[:, :, YT_ON_VECTOR:PATCHES]),
+                by_line_split(y_sb[:, :, YT_ON_VECTOR:PATCHES]),
+                by_line_natural(dt_half[:, cut:HALF]),
+                ALU.mult,
+            )
+            st[step].update(y_sb=y_sb, xt=xt, yy=yy, yt=yt)
+
+        def last_products(step):
+            gx = st[step]["gx"]
+            xx = prod.tile([P, D, PATCHES], F32)
+            xy = prod.tile([P, D, PATCHES], F32)
             nc.scalar.activation(xx[:], by_member(gx[:]), ACT.Square)
-            nc.vector.tensor_tensor(xy[:], by_member(gx[:]), y_sb[:], ALU.mult)
-            nc.gpsimd.tensor_tensor(by_line_split(yt[:]), by_line_split(y_sb[:]), by_line_natural(dt_half), ALU.mult)
-            st[step].update(xt=xt, yy=yy, xy=xy, xx=xx, yt=yt)
+            nc.vector.tensor_tensor(xy[:], by_member(gx[:]), st[step]["y_sb"][:], ALU.mult)
+            st[step].update(xx=xx, xy=xy)
 
         def patch_sums(step):
             sums = psum.tile([P, 4, P], F32, tag="sums", bufs=2)
-            s_yt = psum.tile([P, P], F32, tag="s_yt")
             for n, name in enumerate(("xt", "xx", "yy", "xy")):
                 turn_and_add(sums[:, n, :], [st[step][name][:, d, :] for d in range(D)])
+            st[step].update(s_xt=sums[:, 0, :], s_xx=sums[:, 1, :], s_yy=sums[:, 2, :], s_xy=sums[:, 3, :])
+
+        def patch_sum_yt(step):
+            s_yt = psum.tile([P, P], F32, tag="s_yt")
             turn_and_add(s_yt[:], [st[step]["yt"][:, d, :] for d in range(D)])
-            st[step].update(s_xt=sums[:, 0, :], s_xx=sums[:, 1, :], s_yy=sums[:, 2, :], s_xy=sums[:, 3, :], s_yt=s_yt[:])
+            st[step].update(s_yt=s_yt[:])
 
         def factors(step):
             sxy = small.tile([P, P], F32)
@@ -190,11 +208,14 @@ def tile_picked_ylucas_conf_p_kernel(
             turn_and_add(back[:, 2, :], [st[step]["neg_n1"][:], st[step]["n2"][:]])
             st[step].update(back=back)
 
-        def inverses(step):
-            t, h = divmod(step, 2)
+        def roots(step):
             root = small.tile([P, 2, P], F32, tag="root", bufs=1)
             nc.scalar.activation(root[:], st[step]["back"][:, 0:2, :], ACT.Abs_reciprocal_sqrt, bias=damp[:])
-            nc.scalar.activation(table[t][:, (2 + h) * V : (3 + h) * V], root[:].rearrange("p a v -> p (a v)"), ACT.Square)
+            st[step].update(root=root)
+
+        def inverses(step):
+            t, h = divmod(step, 2)
+            nc.scalar.activation(table[t][:, (2 + h) * V : (3 + h) * V], st[step]["root"][:].rearrange("p a v -> p (a v)"), ACT.Square)
 
         def quotients(step):
             t, h = divmod(step, 2)
@@ -209,22 +230,26 @@ def tile_picked_ylucas_conf_p_kernel(
         stages = (
             (load_dt, -2),
             (gradients, 0),
-            (inverses, 3),
-            (terms, 2),
-            (products, 0),
-            (quotients, 3),
+            (factors, 2),
+            (quotients, 4),
+            (patch_sum_yt, 2),
+            (turn_back, 3),
             (patch_sums, 1),
-            (turn_back, 2),
-            (factors, 1),
+            (first_products, 0),
+            (terms, 2),
+            (roots, 3),
+            (last_products, 0),
+            (inverses, 3),
         )
-        for turn in range(steps + 3):
+        for turn in range(steps + 4):
             for stage, lag in stages:
                 if 0 <= turn - lag < steps:
                     stage(turn - lag)
 
         nc.sync.dma_start(ft_sb[:], ft)
-        w3s = s2_raw[:, 0:N]
-        load_scale_rows((nc.sync,) * 4, w3s, w3_scales[0])
+        w3s = stream.tile([P, N], U8, tag="stream", align_bytes=64)
+        nc.gpsimd.memset(w3s[:].bitcast(I32), 0)
+        load_scale_rows((nc.sync,) * 4, w3s[:], w3_scales[0])
         w3w = stream.tile([P, 2 * N], U8, tag="stream", align_bytes=64)
         nc.sync.dma_start(out=w3w[:].bitcast(I32), in_=w3_words[0].bitcast(I32))
 
@@ -233,17 +258,22 @@ def tile_picked_ylucas_conf_p_kernel(
             nc.scalar.activation(neg_tanh[:, t, :], neg_conf[:, t, :], ACT.Tanh)
             nc.vector.tensor_tensor(table[t][:, 0:V], table[t][:, V : 2 * V], neg_tanh[:, t, :], ALU.mult)
 
+        planes = keep.tile([P, PACK, U], BF16)
+        for t in range(PACK):
+            looked_up = table[t][:].indirect(ft_sb[:])
+            if t % 2 == 0:
+                nc.scalar.activation(planes[:, t, :], looked_up, ACT.Copy)
+            else:
+                nc.vector.tensor_copy(planes[:, t, :], looked_up)
+
         width = U // 2
         for r in range(2):
-            piece = ft_sb[:, r * (width // 16) : (r + 1) * (width // 16)]
-            planes = small.tile([P, PACK, width], BF16)
-            for t in range(PACK - 1):
-                nc.scalar.activation(planes[:, t, :], table[t][:].indirect(piece), ACT.Copy)
-            nc.vector.tensor_copy(planes[:, PACK - 1, :], table[PACK - 1][:].indirect(piece))
+            cols = slice(r * width, (r + 1) * width)
             woven = small.tile([P, width, PACK], BF16, align_bytes=64)
-            nc.vector.tensor_copy(
+            weave = nc.vector.tensor_copy if r == 0 else nc.scalar.copy
+            weave(
                 out=woven[:].rearrange("p (c i) t -> p c t i", i=4),
-                in_=planes[:].rearrange("p t (c i) -> p c t i", i=4),
+                in_=planes[:, :, cols].rearrange("p t (c i) -> p c t i", i=4),
             )
             codes = small.tile([P, width], U32, align_bytes=64)
             scales = small.tile([P, width], U8, align_bytes=64)
@@ -252,12 +282,12 @@ def tile_picked_ylucas_conf_p_kernel(
             nc.tensor.matmul_mx(
                 out=motion[:, 0:width],
                 lhsT=w3w[:].bitcast(FP4X4),
-                lhsT_scale=w3s,
+                lhsT_scale=w3s[:],
                 rhs=codes[:].bitcast(FP8X4),
                 rhs_scale=scales[:],
                 start=True,
                 stop=True,
             )
             result = small.tile([P, width], F32)
-            nc.scalar.copy(result[:], motion[:, 0:width])
-            nc.sync.dma_start(out=out[:, r * width : (r + 1) * width], in_=result[:])
+            nc.vector.tensor_copy(result[:], motion[:, 0:width])
+            nc.sync.dma_start(out=out[:, cols], in_=result[:])

import math
from contextlib import ExitStack

import concourse.mybir as mybir
from concourse.masks import make_identity

K, T, S, D, N, H, V, U = 512, 2048, 1024, 4, 128, 512, 256, 512
FLOPS = 2 * K * H * S * 2 + 2 * H * N * U

F32 = mybir.dt.float32
BF16 = mybir.dt.bfloat16
I32 = mybir.dt.int32
U32 = mybir.dt.uint32
U16 = mybir.dt.uint16
U8 = mybir.dt.uint8
FP8X4 = mybir.dt.float8_e4m3fn_x4
FP4X4 = mybir.dt.float4_e2m1fn_x4
ALU = mybir.AluOpType
ACT = mybir.ActivationFunctionType

P = 128
PACK = 4
HALF = 512
PATCHES = HALF // D
LINE = 4
YT_ON_VECTOR = 32


def load_scale_rows(queues, plane, rows):
    for q, queue in enumerate(queues):
        queue.dma_start(out=plane[32 * q : 32 * q + 4, :].bitcast(I32), in_=rows[4 * q : 4 * q + 4, :].bitcast(I32))


def tile_picked_ylucas_conf_p_kernel(
    tc, x_words, x_scales, w1_words, w1_scales, w2_words, w2_scales, dtm, unit, w3_words, w3_scales, offs, ft, out
):
    nc = tc.nc
    with ExitStack() as ctx:
        keep = ctx.enter_context(tc.tile_pool(name="keep", bufs=1))
        stream = ctx.enter_context(tc.tile_pool(name="stream", bufs=3))
        prod = ctx.enter_context(tc.tile_pool(name="prod", bufs=3))
        small = ctx.enter_context(tc.tile_pool(name="small", bufs=3))
        psum = ctx.enter_context(tc.psum_pool(name="psum", bufs=1))

        offs_sb = keep.tile([P, S // 16], U16)
        ft_sb = keep.tile([P, U // 16], U16)
        xw = keep.tile([P, T], U32, align_bytes=64)
        xs = keep.tile([P, T], U8, align_bytes=64)
        w2_raw = stream.tile([P, 2 * H], U8, tag="stream", align_bytes=64)
        w1_raw = stream.tile([P, 2 * H], U8, tag="stream", align_bytes=64)
        one = stream.tile([P, 1], F32, tag="stream", align_bytes=64)
        s1_raw = keep.tile([P, H], U8, tag="late_words", align_bytes=64)
        s2_raw = keep.tile([P, H], U8, tag="late_bytes", align_bytes=64)
        w_raw = [w1_raw, w2_raw]
        ws_raw = [s1_raw, s2_raw]
        w_dealt = [keep.tile([P, 2 * H], U8, name="w_dealt%d" % i, align_bytes=64) for i in range(2)]
        ws_dealt = [keep.tile([P, H], U8, name="ws_dealt%d" % i, align_bytes=64) for i in range(2)]
        unit_sb = keep.tile([P, PACK], F32)
        ident = keep.tile([P, P], F32)
        damp = keep.tile([P, 1], F32)

        nc.gpsimd.memset(xs[:].bitcast(I32), 0)
        for plane in (s2_raw, s1_raw):
            nc.vector.memset(plane[:].bitcast(I32), 0)
        nc.vector.memset(one[:], 1.0)
        nc.vector.tensor_scalar(damp[:], one[:], -0.3, None, ALU.mult)

        dtm_t = dtm.rearrange("(p t) j -> t p j", t=PACK)
        nc.sync.dma_start(offs_sb[:], offs)
        nc.scalar.dma_start(out=w2_raw[:].bitcast(I32), in_=w2_words[0].bitcast(I32))
        nc.sync.dma_start(out=xw[:].bitcast(I32), in_=x_words[0].rearrange("p c r -> p (c r)").bitcast(I32))
        nc.scalar.dma_start(out=w1_raw[:].bitcast(I32), in_=w1_words[0].bitcast(I32))
        load_scale_rows((nc.sync,) * 4, xs[:], x_scales[0])
        load_scale_rows((nc.scalar,) * 4, s2_raw[:], w2_scales[0])
        load_scale_rows((nc.sync, nc.scalar, nc.sync, nc.scalar), s1_raw[:], w1_scales[0])
        make_identity(nc, ident[:])
        nc.gpsimd.dma_start(out=unit_sb[:], in_=unit.rearrange("(p t) o -> p (t o)", t=PACK))

        for i in (1, 0):
            nc.vector.tensor_copy(
                out=w_dealt[i][:].rearrange("p (t m b) -> p t m b", t=PACK, b=2),
                in_=w_raw[i][:].rearrange("p (m t b) -> p t m b", t=PACK, b=2),
            )
        for i in (1, 0):
            nc.vector.tensor_copy(
                out=ws_dealt[i][:].rearrange("p (t m) -> p t m", t=PACK),
                in_=ws_raw[i][:].rearrange("p (m t) -> p t m", t=PACK),
            )

        xg = [keep.tile([P, HALF], U32, name="xg", tag=tag, align_bytes=64) for tag in ("first_words", "late_words")]
        sg = [keep.tile([P, HALF], U8, name="sg", tag=tag, align_bytes=64) for tag in ("first_bytes", "late_bytes")]
        for h in range(2):
            piece = offs_sb[:, h * (HALF // 16) : (h + 1) * (HALF // 16)]
            nc.vector.tensor_copy(sg[h][:], xs[:].indirect(piece))
            nc.vector.tensor_copy(xg[h][:], xw[:].indirect(piece))


        def gradient(i, t, h, bank):
            nc.tensor.matmul_mx(
                out=bank[:],
                lhsT=w_dealt[i][:, 2 * P * t : 2 * P * (t + 1)].bitcast(FP4X4),
                lhsT_scale=ws_dealt[i][:, P * t : P * (t + 1)],
                rhs=xg[h][:].bitcast(FP8X4),
                rhs_scale=sg[h][:],
                start=True,
                stop=True,
            )

        def turn_and_add(dst, terms):
            for n, term in enumerate(terms):
                nc.tensor.matmul(dst, term, ident[:], start=(n == 0), stop=(n == len(terms) - 1), is_transpose=True)

        def by_member(ap):
            return ap.rearrange("p (v d) -> p d v", d=D)

        def by_line_natural(ap):
            return ap.rearrange("p (c i d) -> p c d i", i=LINE, d=D)

        def by_line_split(ap):
            return ap.rearrange("p d (c i) -> p c d i", i=LINE)

        neg_conf = keep.tile([P, PACK, V], F32)
        table = [keep.tile([P, 4 * V], F32, name="table%d" % t) for t in range(PACK)]

        steps = 2 * PACK
        st = [dict() for step in range(steps)]

        def load_dt(step):
            t, h = divmod(step, 2)
            dt_half = stream.tile([P, HALF], F32, tag="stream", align_bytes=64)
            nc.sync.dma_start(out=dt_half[:], in_=dtm_t[t, :, h * HALF : (h + 1) * HALF])
            st[step].update(dt=dt_half[:])

        def gradients(step):
            t, h = divmod(step, 2)
            gy = psum.tile([P, HALF], F32, tag="gy")
            gx = psum.tile([P, HALF], F32, tag="gx", bufs=2)
            gradient(1, t, h, gy)
            gradient(0, t, h, gx)
            st[step].update(gx=gx, gy=gy)

        def first_products(step):
            gx, gy, dt_half = st[step]["gx"], st[step]["gy"], st[step]["dt"]
            y_sb = prod.tile([P, D, PATCHES], F32)
            xt = prod.tile([P, D, PATCHES], F32)
            yy = prod.tile([P, D, PATCHES], F32)
            yt = prod.tile([P, D, PATCHES], F32)
            nc.scalar.copy(y_sb[:], by_member(gy[:]))
            nc.vector.tensor_tensor(by_line_split(xt[:]), by_line_natural(gx[:]), by_line_natural(dt_half), ALU.mult)
            nc.scalar.activation(yy[:, 0:1, :], by_member(gy[:])[:, 0:1, :], ACT.Square)
            nc.gpsimd.tensor_tensor(yy[:, 1:D, :], y_sb[:, 1:D, :], y_sb[:, 1:D, :], ALU.mult)
            cut = D * YT_ON_VECTOR
            nc.vector.tensor_tensor(
                by_line_split(yt[:, :, 0:YT_ON_VECTOR]), by_line_natural(gy[:, 0:cut]), by_line_natural(dt_half[:, 0:cut]), ALU.mult
            )
            nc.gpsimd.tensor_tensor(
                by_line_split(yt[:, :, YT_ON_VECTOR:PATCHES]),
                by_line_split(y_sb[:, :, YT_ON_VECTOR:PATCHES]),
                by_line_natural(dt_half[:, cut:HALF]),
                ALU.mult,
            )
            st[step].update(y_sb=y_sb, xt=xt, yy=yy, yt=yt)

        def last_products(step):
            gx = st[step]["gx"]
            xx = prod.tile([P, D, PATCHES], F32)
            xy = prod.tile([P, D, PATCHES], F32)
            nc.scalar.activation(xx[:], by_member(gx[:]), ACT.Square)
            nc.vector.tensor_tensor(xy[:], by_member(gx[:]), st[step]["y_sb"][:], ALU.mult)
            st[step].update(xx=xx, xy=xy)

        def patch_sums(step):
            sums = psum.tile([P, 4, P], F32, tag="sums", bufs=2)
            for n, name in enumerate(("xt", "xx", "yy", "xy")):
                turn_and_add(sums[:, n, :], [st[step][name][:, d, :] for d in range(D)])
            st[step].update(s_xt=sums[:, 0, :], s_xx=sums[:, 1, :], s_yy=sums[:, 2, :], s_xy=sums[:, 3, :])

        def patch_sum_yt(step):
            s_yt = psum.tile([P, P], F32, tag="s_yt")
            turn_and_add(s_yt[:], [st[step]["yt"][:, d, :] for d in range(D)])
            st[step].update(s_yt=s_yt[:])

        def factors(step):
            sxy = small.tile([P, P], F32)
            damped = small.tile([P, P], F32)
            neg_syy = small.tile([P, P], F32)
            nc.scalar.activation(neg_syy[:], st[step]["s_yy"], ACT.Copy, bias=-0.5, scale=-1.0)
            nc.scalar.activation(damped[:], st[step]["s_xy"], ACT.Square, scale=math.sqrt(0.8))
            nc.scalar.copy(sxy[:], st[step]["s_xy"])
            st[step].update(sxy=sxy, damped=damped, neg_syy=neg_syy)

        def terms(step):
            neg_n1 = small.tile([P, P], F32)
            neg_ab = small.tile([P, P], F32)
            trace = small.tile([P, P], F32)
            n2 = small.tile([P, P], F32)
            neg_syy = st[step]["neg_syy"]
            nc.vector.scalar_tensor_tensor(neg_ab[:], st[step]["s_xx"], 0.5, neg_syy[:], ALU.add, ALU.mult)
            nc.vector.scalar_tensor_tensor(trace[:], st[step]["s_xx"], 0.8, neg_syy[:], ALU.add, ALU.subtract)
            nc.vector.tensor_tensor(neg_n1[:], st[step]["s_xt"], neg_syy[:], ALU.mult)
            nc.vector.tensor_tensor(n2[:], st[step]["s_yt"], st[step]["sxy"][:], ALU.mult)
            st[step].update(neg_n1=neg_n1, neg_ab=neg_ab, trace=trace, n2=n2)

        def turn_back(step):
            back = psum.tile([P, 3, P], F32, tag="back", bufs=2)
            turn_and_add(back[:, 0, :], [st[step]["neg_ab"][:], st[step]["damped"][:]])
            turn_and_add(back[:, 1, :], [st[step]["trace"][:]])
            turn_and_add(back[:, 2, :], [st[step]["neg_n1"][:], st[step]["n2"][:]])
            st[step].update(back=back)

        def roots(step):
            root = small.tile([P, 2, P], F32, tag="root", bufs=1)
            nc.scalar.activation(root[:], st[step]["back"][:, 0:2, :], ACT.Abs_reciprocal_sqrt, bias=damp[:])
            st[step].update(root=root)

        def inverses(step):
            t, h = divmod(step, 2)
            nc.scalar.activation(table[t][:, (2 + h) * V : (3 + h) * V], st[step]["root"][:].rearrange("p a v -> p (a v)"), ACT.Square)

        def quotients(step):
            t, h = divmod(step, 2)
            back = st[step]["back"]
            inv = table[t][:, (2 + h) * V : (3 + h) * V]
            neg_u = table[t][:, V + h * P : V + (h + 1) * P]
            nc.vector.scalar_tensor_tensor(neg_conf[:, t, h * P : (h + 1) * P], back[:, 0, :], -0.3, inv[:, P : 2 * P], ALU.add, ALU.mult)
            nc.vector.scalar_tensor_tensor(neg_u, back[:, 2, :], unit_sb[:, t : t + 1], inv[:, 0:P], ALU.mult, ALU.mult)

        load_dt(0)
        load_dt(1)
        stages = (
            (load_dt, -2),
            (gradients, 0),
            (factors, 2),
            (quotients, 4),
            (patch_sum_yt, 2),
            (turn_back, 3),
            (patch_sums, 1),
            (first_products, 0),
            (terms, 2),
            (roots, 3),
            (last_products, 0),
            (inverses, 3),
        )
        for turn in range(steps + 4):
            for stage, lag in stages:
                if 0 <= turn - lag < steps:
                    stage(turn - lag)

        nc.sync.dma_start(ft_sb[:], ft)
        w3s = stream.tile([P, N], U8, tag="stream", align_bytes=64)
        nc.gpsimd.memset(w3s[:].bitcast(I32), 0)
        load_scale_rows((nc.sync,) * 4, w3s[:], w3_scales[0])
        w3w = stream.tile([P, 2 * N], U8, tag="stream", align_bytes=64)
        nc.sync.dma_start(out=w3w[:].bitcast(I32), in_=w3_words[0].bitcast(I32))

        neg_tanh = small.tile([P, PACK, V], F32, tag="root", bufs=1)
        for t in range(PACK):
            nc.scalar.activation(neg_tanh[:, t, :], neg_conf[:, t, :], ACT.Tanh)
            nc.vector.tensor_tensor(table[t][:, 0:V], table[t][:, V : 2 * V], neg_tanh[:, t, :], ALU.mult)

        planes = keep.tile([P, PACK, U], BF16)
        for t in range(PACK):
            looked_up = table[t][:].indirect(ft_sb[:])
            if t % 2 == 0:
                nc.scalar.activation(planes[:, t, :], looked_up, ACT.Copy)
            else:
                nc.vector.tensor_copy(planes[:, t, :], looked_up)

        width = U // 2
        for r in range(2):
            cols = slice(r * width, (r + 1) * width)
            woven = small.tile([P, width, PACK], BF16, align_bytes=64)
            weave = nc.vector.tensor_copy if r == 0 else nc.scalar.copy
            weave(
                out=woven[:].rearrange("p (c i) t -> p c t i", i=4),
                in_=planes[:, :, cols].rearrange("p t (c i) -> p c t i", i=4),
            )
            codes = small.tile([P, width], U32, align_bytes=64)
            scales = small.tile([P, width], U8, align_bytes=64)
            nc.vector.quantize_mx(out=codes[:].bitcast(FP8X4), scales=scales[:], in_=woven[:].rearrange("p c t -> p (c t)"))
            motion = psum.tile([P, HALF], F32, tag="gx", bufs=2)
            nc.tensor.matmul_mx(
                out=motion[:, 0:width],
                lhsT=w3w[:].bitcast(FP4X4),
                lhsT_scale=w3s[:],
                rhs=codes[:].bitcast(FP8X4),
                rhs_scale=scales[:],
                start=True,
                stop=True,
            )
            result = small.tile([P, width], F32)
            nc.vector.tensor_copy(result[:], motion[:, 0:width])
            nc.sync.dma_start(out=out[:, cols], in_=result[:])
